import numpy as np
import ml_dtypes


def mxq(x, axis, fmt="e4m3"):
    dtype, down = {"e4m3": (ml_dtypes.float8_e4m3fn, 7), "e5m2": (ml_dtypes.float8_e5m2, 14)}[fmt]
    v = np.moveaxis(np.asarray(x, np.float32).astype(ml_dtypes.bfloat16).astype(np.float64), axis, -1)
    blocks = v.reshape(v.shape[:-1] + (-1, 32))
    amax = np.abs(blocks).max(-1, keepdims=True)
    byte = np.maximum(np.where(amax > 0, np.frexp(amax)[1] - 1 + 127, 0) - down, 1)
    scale = np.exp2(byte - 127.0)
    codes = (blocks / scale).astype(np.float32).astype(dtype).astype(np.float64)
    return np.moveaxis((codes * scale).reshape(v.shape), -1, axis)


WIDE = False


def mx_kscale(k):
    if not WIDE:
        return np.ones(k)
    levels = np.array([10, -10, 5, -5, 0])
    if k % 512:
        return np.exp2(np.random.permutation(np.resize(levels, k // 32))).repeat(32)
    a = np.empty((k // 512, 16))
    for p in range(k // 512):
        a[p, :8] = np.random.permutation(np.resize(levels, 8))
        for g in range(8):
            far = levels[np.abs(levels - a[p, g]) >= 10]
            a[p, g + 8] = far[np.random.randint(len(far))]
    return np.exp2(a.ravel()).repeat(32)


def f64(x):
    return np.asarray(x).astype(np.float64)


def striped(idx):
    return np.tile(np.asarray(idx).reshape(-1, 16).T, (8, 1)).astype(np.uint16)


def unstriped(offs):
    return offs[:16].T.reshape(-1).astype(np.int64)


E2M1 = np.array([0.0, 0.5, 1.0, 1.5, 2.0, 3.0, 4.0, 6.0, -0.0, -0.5, -1.0, -1.5, -2.0, -3.0, -4.0, -6.0])


def pack_weight(w, fmt):
    k, n = w.shape
    w = f64(np.asarray(w, np.float32).astype(ml_dtypes.bfloat16)).reshape(k // 32, 32, n)
    amax = np.abs(w).max(1)
    if fmt == "e4m3":
        byte = np.frexp(amax)[1] - 1 + 127 - 7
    else:
        mant, ex = np.frexp(amax / 6.0)
        byte = np.where(mant > 0.5, ex, ex - 1) + 127
    byte = np.clip(np.where(amax > 0, byte, 1), 1, 254)
    scaled = (w * np.exp2(127.0 - byte)[:, None, :]).reshape(k, n).astype(np.float32)
    by_word = np.ascontiguousarray(scaled.reshape(k // 512, 128, 4, n).transpose(0, 1, 3, 2))
    if fmt == "e4m3":
        words = by_word.astype(ml_dtypes.float8_e4m3fn).view(np.uint8)
    else:
        c = by_word.astype(ml_dtypes.float4_e2m1fn).view(np.uint8) & 0xF
        words = (c[..., 0::2] | (c[..., 1::2] << 4)).reshape(k // 512, 128, 2 * n)
    return np.ascontiguousarray(words), np.ascontiguousarray(byte.astype(np.uint8).reshape(k // 512, 16, n))


def unpack_weight(words, scales, fmt):
    g, _, n = scales.shape
    words = np.ascontiguousarray(words).reshape(g, 128, n, -1)
    if fmt == "e4m3":
        vals = words.view(ml_dtypes.float8_e4m3fn).astype(np.float64)
    else:
        nib = np.empty((g, 128, n, 4), np.uint8)
        nib[..., 0::2] = words & 0xF
        nib[..., 1::2] = words >> 4
        vals = E2M1[nib]
    vals = vals * np.repeat(np.exp2(scales.astype(np.float64) - 127.0), 8, axis=1)[..., None]
    return vals.transpose(0, 1, 3, 2).reshape(g * 512, n)


D, K, R, T, I, Q, G = 512, 512, 512, 2048, 512, 128, 64


def setup_inputs():
    n = np.random.standard_normal
    idx = np.random.permutation(T)[:I]
    fd = mx_kscale(D)
    fk = mx_kscale(K)
    fi = mx_kscale(I)
    keysp = pack_weight(n((D, T)) / fd[:, None], "e2m1")
    tabp = pack_weight(n((K, T)) / fk[:, None], "e2m1")
    return {
        "query": (n((D, Q)) * 0.6 / np.sqrt(D) * fd[:, None]).astype(np.float32),
        "keys_words": keysp[0],
        "keys_scales": keysp[1],
        "sharp": (np.random.uniform(1.0, 3.0, (Q, 1))).astype(np.float32),
        "tab_words": tabp[0],
        "tab_scales": tabp[1],
        "w1": (n((K, R)) * 1 / np.sqrt(K) * fk[:, None]).astype(np.float32),
        "temper": (np.random.uniform(0.4, 1.0, (R, 1))).astype(np.float32),
        "os": (np.random.uniform(4.0, 16.0, (1, I)) * fi).astype(np.float32),
        "vs": (np.random.uniform(0.5, 2.0, (1, I)) / fi).astype(np.float32),
        "offs": striped(idx),
    }


def reference(query, keys_words, keys_scales, sharp, tab_words, tab_scales, w1, temper, os, vs, offs):
    idx = unstriped(offs)
    keysu = unpack_weight(keys_words, keys_scales, "e2m1")
    tabu = unpack_weight(tab_words, tab_scales, "e2m1")
    queryq = mxq(f64(query), 0, "e4m3")
    keysidxg = keysu[:, idx]
    a = queryq.T @ keysidxg
    p = np.exp(a)
    s = p.reshape(Q, G, I // G).sum(axis=2)
    ms = a.reshape(Q, G, I // G).mean(axis=2) * f64(sharp)
    pg = np.exp(ms - np.max(ms, axis=1, keepdims=True))
    z = np.sum(pg, axis=1, keepdims=True)
    sh = pg / z / s
    rr = np.repeat(sh, I // G, axis=1)
    w = p * rr
    w1q = mxq(f64(w1), 0, "e4m3")
    tabidxg = tabu[:, idx]
    zh = w1q.T @ tabidxg
    ht = np.exp(zh * f64(temper))
    mz = ht.reshape(R, G, I // G).sum(axis=2)
    mzr = np.repeat(mz, I // G, axis=1)
    hv = ht / mzr * 4.0
    wo1 = w * f64(os)
    wt1 = wo1.T
    hw = hv * f64(vs)
    ht1 = hw.T
    wt1q = mxq(wt1, 0, "e4m3")
    ht1q = mxq(ht1, 0, "e4m3")
    o = wt1q.T @ ht1q
    return o

@@ -1,0 +1,206 @@
+from contextlib import ExitStack
+
+import concourse.mybir as mybir
+from concourse.masks import make_identity
+
+F32 = mybir.dt.float32
+BF16 = mybir.dt.bfloat16
+I32 = mybir.dt.int32
+U32 = mybir.dt.uint32
+U16 = mybir.dt.uint16
+U8 = mybir.dt.uint8
+FP8X4 = mybir.dt.float8_e4m3fn_x4
+FP4X4 = mybir.dt.float4_e2m1fn_x4
+ALU = mybir.AluOpType
+ACT = mybir.ActivationFunctionType
+AX = mybir.AxisListType
+
+P = 128
+PACK = 4
+T = 2048
+I = 512
+R = 512
+Q = 128
+G = 64
+NCH = R // P
+FLOPS = 2 * (512 * Q * I + 512 * R * I + I * Q * R)
+
+
+def tile_attend_lrshared_bygroup_kernel(tc, query, keys_words, keys_scales, sharp, tab_words, tab_scales, w1, temper, os_in, vs_in, offs, out):
+    nc = tc.nc
+    with ExitStack() as ctx:
+        held = ctx.enter_context(tc.tile_pool(name="held", bufs=1))
+        psum = ctx.enter_context(tc.psum_pool(name="psum", bufs=1))
+
+        def sb(name, shape, dt):
+            return held.tile(shape, dt, name=name, align_bytes=64)
+
+        offsets = held.tile([P, I // 16], U16, name="offsets")
+        tab_w = sb("tab_w", [P, T], U16)
+        key_w = sb("key_w", [P, T], U16)
+        tab_s = sb("tab_s", [P, T], U8)
+        key_s = sb("key_s", [P, T], U8)
+        w_raw = [sb("w_raw0", [P, PACK, 2 * P], F32)]
+        shp = sb("shp", [P, 1], F32)
+        vs_t = sb("vs_t", [P, PACK], F32)
+        os_t = sb("os_t", [P, PACK], F32)
+        ident = sb("ident", [P, P], F32)
+        recs = sb("recs", [P, NCH, 2 * G + 16], F32)
+
+        nc.vector.memset(tab_s[:].bitcast(I32), 0)
+        nc.gpsimd.memset(key_s[:].bitcast(I32), 0)
+        seed = held.tile([P, 1], F32, name="seed", tag="late_q", align_bytes=64)
+        warm = held.tile([P, 1], F32, name="warm", tag="late_w", align_bytes=64)
+        warm_sum = held.tile([P, 1], F32, name="warm_sum", tag="late_t", align_bytes=64)
+        nc.vector.memset(seed[:], 0.0)
+        nc.vector.memset(recs[:], 0.0)
+
+        w1v = w1.rearrange("(p j) r -> p j r", j=PACK)
+        nc.sync.dma_start(offsets[:], offs)
+        for j in range(4):
+            nc.scalar.dma_start(tab_s[j:P:32, :].bitcast(I32), tab_scales[0, j:16:4, :].bitcast(I32))
+        nc.sync.dma_start(tab_w[:].bitcast(I32), tab_words[0].bitcast(I32))
+        nc.scalar.activation(warm[:], seed[:], ACT.Exp, accum_out=warm_sum[:])
+        nc.sync.dma_start(w_raw[0][:], w1v[:, :, 0 : 2 * P])
+        nc.sync.dma_start(key_w[:].bitcast(I32), keys_words[0].bitcast(I32))
+        for j in range(4):
+            nc.gpsimd.dma_start(key_s[j:P:32, :].bitcast(I32), keys_scales[0, j:16:4, :].bitcast(I32))
+        temp = held.tile([P, NCH], F32, name="temp", tag="late_t", align_bytes=64)
+        q_raw = held.tile([P, PACK, Q], F32, name="q_raw", tag="late_q", align_bytes=64)
+        w_raw.append(held.tile([P, PACK, 2 * P], F32, name="w_raw1", tag="late_w", align_bytes=64))
+        with nc.allow_non_contiguous_dma(reason="one value a partition"):
+            nc.sync.dma_start(temp[:], temper.rearrange("(c p) o -> p (c o)", p=P))
+        nc.sync.dma_start(q_raw[:], query.rearrange("(p j) q -> p j q", j=PACK))
+        nc.sync.dma_start(w_raw[1][:], w1v[:, :, 2 * P : 4 * P])
+        make_identity(nc, ident[:])
+        nc.gpsimd.dma_start(vs_t[:], vs_in.rearrange("o (p t) -> p (o t)", t=PACK))
+        nc.gpsimd.dma_start(shp[:], sharp)
+        nc.gpsimd.dma_start(os_t[:], os_in.rearrange("o (p t) -> p (o t)", t=PACK))
+        vs4 = sb("vs4", [P, PACK], F32)
+        nc.scalar.activation(vs4[:], vs_t[:], ACT.Copy, scale=4.0)
+        nshp = sb("nshp", [P, 1], F32)
+        nc.scalar.activation(nshp[:], shp[:], ACT.Copy, scale=-0.125)
+
+        banks = [psum.tile([P, I], F32, name="bank%d" % c) for c in range(NCH + 1)]
+
+        def gather(name, window, dt):
+            g = sb(name, [P, I], dt)
+            nc.vector.tensor_copy(g[:], window[:].indirect(offsets[:]))
+            return g
+
+        def weave(name, raw):
+            g = sb(name, [P, P * PACK], BF16)
+            nc.scalar.activation(
+                g[:].rearrange("p (c i t) -> p c t i", i=4, t=PACK),
+                raw.rearrange("p t (c i) -> p c t i", i=4),
+                ACT.Copy,
+            )
+            return g
+
+        def quantise(name, g):
+            codes = sb(name + "_c", [P, P], U32)
+            scales = sb(name + "_s", [P, P], U8)
+            nc.vector.quantize_mx(out=codes[:].bitcast(FP8X4), scales=scales[:], in_=g[:])
+            return codes, scales
+
+        def score(c, cs, words, scales):
+            nc.tensor.matmul_mx(out=banks[c][:], lhsT=cs[0][:].bitcast(FP8X4), lhsT_scale=cs[1][:],
+                                rhs=words[:].bitcast(FP4X4), rhs_scale=scales[:], start=True, stop=True)
+
+        def expo(c, scale):
+            e = sb("e%d" % c, [P, PACK, P], F32)
+            nc.scalar.activation(e[:], banks[c][:].rearrange("p (m t) -> p t m", t=PACK), ACT.Exp, scale=scale)
+            return e
+
+        def group_sum(c, e):
+            s = sb("s%d" % c, [P, G], F32)
+            nc.vector.tensor_reduce(s[:], e[:].rearrange("p t (g h) -> p g t h", h=2), AX.XY, ALU.add)
+            return s
+
+        def turn(c, e, factor):
+            for t in range(PACK):
+                nc.tensor.transpose(banks[c][:, t * P : (t + 1) * P], e[:, t, :], ident[:])
+            v = sb("v%d" % c, [P, PACK, P], F32)
+            for t in range(PACK):
+                nc.scalar.activation(v[:, t, :], banks[c][:, t * P : (t + 1) * P], ACT.Copy, scale=factor[:, t : t + 1])
+            return v
+
+        def finish(c, v):
+            g = sb("f%d" % c, [P, P * PACK], BF16)
+            nc.vector.tensor_tensor(
+                g[:].rearrange("p (c i t) -> p c t i", i=4, t=PACK),
+                v[:].rearrange("p t (c i) -> p c t i", i=4),
+                banks[c][:, 0:P].rearrange("p (c i) -> p c i", i=4).unsqueeze(2).to_broadcast([P, P // 4, PACK, 4]),
+                ALU.mult,
+            )
+            return quantise("fq%d" % c, g)
+
+        def hidden_norm(c, s):
+            nc.vector.reciprocal(recs[:, c, 1 : 2 * G + 1 : 2], s[:])
+            nc.tensor.matmul(banks[c][:, 0:P], recs[:, c, 1 : P + 1], ident[:], start=True, stop=False, is_transpose=True)
+            nc.tensor.matmul(banks[c][:, 0:P], recs[:, c, 0:P], ident[:], start=False, stop=True, is_transpose=True)
+
+        def result(c, wq, hq):
+            nc.tensor.matmul_mx(out=banks[c][:, P : 2 * P], lhsT=wq[0][:].bitcast(FP8X4), lhsT_scale=wq[1][:],
+                                rhs=hq[0][:].bitcast(FP8X4), rhs_scale=hq[1][:], start=True, stop=True)
+            o = sb("o%d" % c, [P, P], F32)
+            nc.scalar.copy(o[:], banks[c][:, P : 2 * P])
+            nc.sync.dma_start(out[:, c * P : (c + 1) * P], o[:])
+
+        tab_gs = gather("tab_gs", tab_s, U8)
+        tab_gw = gather("tab_gw", tab_w, U16)
+        es = {}
+        for c in range(2):
+            wq = quantise("wq%d" % c, weave("wg%d" % c, w_raw[0][:, :, c * P : (c + 1) * P]))
+            score(c, wq, tab_gw, tab_gs)
+            es[c] = expo(c, temp[:, c : c + 1])
+        key_gs = gather("key_gs", key_s, U8)
+        key_gw = gather("key_gw", key_w, U16)
+        qq = quantise("qq", weave("qg", q_raw[:]))
+        score(NCH, qq, key_gw, key_gs)
+        es[NCH] = expo(NCH, 1.0)
+        for c in range(2, NCH):
+            wq = quantise("wq%d" % c, weave("wg%d" % c, w_raw[1][:, :, (c - 2) * P : (c - 1) * P]))
+            score(c, wq, tab_gw, tab_gs)
+            es[c] = expo(c, temp[:, c : c + 1])
+
+        s0 = group_sum(0, es[0])
+        v0 = turn(0, es[0], vs4)
+        hidden_norm(0, s0)
+
+        sa = sb("sa", [P, G], F32)
+        nc.vector.tensor_reduce(sa[:], banks[NCH][:].rearrange("p (g u) -> p g u", u=8), AX.X, ALU.add)
+        sp = group_sum(NCH, es[NCH])
+        nms = sb("nms", [P, G], F32)
+        low = sb("low", [P, 1], F32)
+        nc.vector.tensor_scalar(nms[:], sa[:], nshp[:, 0:1], 3.0e38, ALU.mult, ALU.min, accum_out=low[:])
+        pg = sb("pg", [P, G], F32)
+        z = sb("z", [P, 1], F32)
+        nc.scalar.activation(pg[:], nms[:], ACT.Exp, bias=low[:, 0:1], scale=-1.0, accum_out=z[:])
+        vw = turn(NCH, es[NCH], os_t)
+        rs = sb("rs", [P, G], F32)
+        nc.vector.reciprocal(rs[:], sp[:])
+        hq0 = finish(0, v0)
+        rz = sb("rz", [P, 1], F32)
+        nc.vector.reciprocal(rz[:], z[:])
+        s1 = group_sum(1, es[1])
+        v1 = turn(1, es[1], vs4)
+        sh = sb("sh", [P, G, 2], F32)
+        nc.vector.scalar_tensor_tensor(sh[:], pg[:].unsqueeze(2).to_broadcast([P, G, 2]), rz[:, 0:1],
+                                       rs[:].unsqueeze(2).to_broadcast([P, G, 2]), ALU.mult, ALU.mult)
+        nc.tensor.transpose(banks[NCH][:, 0:P], sh[:].rearrange("p g h -> p (g h)"), ident[:])
+        hidden_norm(1, s1)
+        s2 = group_sum(2, es[2])
+        v2 = turn(2, es[2], vs4)
+        wq = finish(NCH, vw)
+        result(0, wq, hq0)
+        hq1 = finish(1, v1)
+        result(1, wq, hq1)
+        hidden_norm(2, s2)
+        s3 = group_sum(3, es[3])
+        v3 = turn(3, es[3], vs4)
+        hidden_norm(3, s3)
+        hq2 = finish(2, v2)
+        result(2, wq, hq2)
+        hq3 = finish(3, v3)
+        result(3, wq, hq3)

@@ -40,167 +40,239 @@ def tile_attend_lrshared_bygroup_kernel(tc, query, keys_words, keys_scales, shar
         key_w = sb("key_w", [P, T], U16)
         tab_s = sb("tab_s", [P, T], U8)
         key_s = sb("key_s", [P, T], U8)
-        w_raw = [sb("w_raw0", [P, PACK, 2 * P], F32)]
+        w_raw = [sb("w_raw%d" % h, [P, PACK, 2 * P], F32) for h in range(2)]
+        q_raw = sb("q_raw", [P, PACK, Q], F32)
+        temp = sb("temp", [P, NCH], F32)
         shp = sb("shp", [P, 1], F32)
         vs_t = sb("vs_t", [P, PACK], F32)
         os_t = sb("os_t", [P, PACK], F32)
+        vs4 = sb("vs4", [P, PACK], F32)
+        nshp = sb("nshp", [P, 1], F32)
         ident = sb("ident", [P, P], F32)
         recs = sb("recs", [P, NCH, 2 * G + 16], F32)
-
-        nc.vector.memset(tab_s[:].bitcast(I32), 0)
-        nc.gpsimd.memset(key_s[:].bitcast(I32), 0)
-        seed = held.tile([P, 1], F32, name="seed", tag="late_q", align_bytes=64)
-        warm = held.tile([P, 1], F32, name="warm", tag="late_w", align_bytes=64)
-        warm_sum = held.tile([P, 1], F32, name="warm_sum", tag="late_t", align_bytes=64)
-        nc.vector.memset(seed[:], 0.0)
-        nc.vector.memset(recs[:], 0.0)
-
         w1v = w1.rearrange("(p j) r -> p j r", j=PACK)
+        nc.gpsimd.memset(tab_s[:].bitcast(I32), 0)
+        nc.vector.memset(recs[:], 0.0)
+        nc.vector.memset(key_s[:].bitcast(I32), 0)
+        make_identity(nc, ident[:])
         nc.sync.dma_start(offsets[:], offs)
+        nc.scalar.dma_start(shp[:], sharp)
         for j in range(4):
             nc.scalar.dma_start(tab_s[j:P:32, :].bitcast(I32), tab_scales[0, j:16:4, :].bitcast(I32))
+        nc.sync.dma_start(vs_t[:], vs_in.rearrange("o (p t) -> p (o t)", t=PACK))
         nc.sync.dma_start(tab_w[:].bitcast(I32), tab_words[0].bitcast(I32))
-        nc.scalar.activation(warm[:], seed[:], ACT.Exp, accum_out=warm_sum[:])
         nc.sync.dma_start(w_raw[0][:], w1v[:, :, 0 : 2 * P])
-        nc.sync.dma_start(key_w[:].bitcast(I32), keys_words[0].bitcast(I32))
-        for j in range(4):
-            nc.gpsimd.dma_start(key_s[j:P:32, :].bitcast(I32), keys_scales[0, j:16:4, :].bitcast(I32))
-        temp = held.tile([P, NCH], F32, name="temp", tag="late_t", align_bytes=64)
-        q_raw = held.tile([P, PACK, Q], F32, name="q_raw", tag="late_q", align_bytes=64)
-        w_raw.append(held.tile([P, PACK, 2 * P], F32, name="w_raw1", tag="late_w", align_bytes=64))
-        with nc.allow_non_contiguous_dma(reason="one value a partition"):
-            nc.sync.dma_start(temp[:], temper.rearrange("(c p) o -> p (c o)", p=P))
         nc.sync.dma_start(q_raw[:], query.rearrange("(p j) q -> p j q", j=PACK))
         nc.sync.dma_start(w_raw[1][:], w1v[:, :, 2 * P : 4 * P])
-        make_identity(nc, ident[:])
-        nc.gpsimd.dma_start(vs_t[:], vs_in.rearrange("o (p t) -> p (o t)", t=PACK))
-        nc.gpsimd.dma_start(shp[:], sharp)
-        nc.gpsimd.dma_start(os_t[:], os_in.rearrange("o (p t) -> p (o t)", t=PACK))
-        vs4 = sb("vs4", [P, PACK], F32)
-        nc.scalar.activation(vs4[:], vs_t[:], ACT.Copy, scale=4.0)
-        nshp = sb("nshp", [P, 1], F32)
-        nc.scalar.activation(nshp[:], shp[:], ACT.Copy, scale=-0.125)
+        with nc.allow_non_contiguous_dma(reason="one value a partition"):
+            nc.sync.dma_start(temp[:], temper.rearrange("(c p) o -> p (c o)", p=P))
+        for j in range(4):
+            nc.scalar.dma_start(key_s[j:P:32, :].bitcast(I32), keys_scales[0, j:16:4, :].bitcast(I32))
+        nc.sync.dma_start(key_w[:].bitcast(I32), keys_words[0].bitcast(I32))
+        nc.sync.dma_start(os_t[:], os_in.rearrange("o (p t) -> p (o t)", t=PACK))
+        nc.gpsimd.tensor_scalar(vs4[:], vs_t[:], 4.0, 0.0, ALU.mult, ALU.add)
+        nc.gpsimd.tensor_scalar(nshp[:], shp[:], -0.125, 0.0, ALU.mult, ALU.add)
 
         banks = [psum.tile([P, I], F32, name="bank%d" % c) for c in range(NCH + 1)]
+        sums = [psum.tile([P, 2 * P], F32, name="sums%d" % u) for u in range(3)]
+        es = [sb("e%d" % u, [P, PACK, 2 * P], F32) for u in range(3)]
+        vv = [sb("v%d" % u, [P, PACK, 2 * P], F32) for u in range(2)]
+        vw = sb("vw", [P, PACK, P], F32)
+        gs = [sb("gs%d" % u, [P, 2, G], F32) for u in range(3)]
+        nms = sb("nms", [P, G], F32)
+        low = sb("low", [P, 1], F32)
+        pg = sb("pg", [P, G], F32)
+        z = sb("z", [P, 1], F32)
+        rs = sb("rs", [P, G], F32)
+        rz = sb("rz", [P, 1], F32)
+        sh = sb("sh", [P, G, 2], F32)
+        got = {}
 
-        def gather(name, window, dt):
-            g = sb(name, [P, I], dt)
-            nc.vector.tensor_copy(g[:], window[:].indirect(offsets[:]))
-            return g
+        def tagged(name, shape, dt, tag):
+            return held.tile(shape, dt, name=name, tag=tag or name, align_bytes=64)
 
-        def weave(name, raw):
-            g = sb(name, [P, P * PACK], BF16)
-            nc.scalar.activation(
-                g[:].rearrange("p (c i t) -> p c t i", i=4, t=PACK),
-                raw.rearrange("p t (c i) -> p c t i", i=4),
-                ACT.Copy,
-            )
-            return g
+        def gather(name, window, dt, tag=None):
+            got[name] = tagged(name, [P, I], dt, tag)
+            nc.vector.tensor_copy(got[name][:], window[:].indirect(offsets[:]))
 
-        def quantise(name, g):
-            codes = sb(name + "_c", [P, P], U32)
-            scales = sb(name + "_s", [P, P], U8)
-            nc.vector.quantize_mx(out=codes[:].bitcast(FP8X4), scales=scales[:], in_=g[:])
-            return codes, scales
+        def weave(c, copy, tag=None):
+            raw = q_raw[:] if c == NCH else w_raw[c // 2][:, :, (c % 2) * P : (c % 2 + 1) * P]
+            g = tagged("wg%d" % c, [P, P * PACK], BF16, tag)
+            copy(g[:].rearrange("p (c i t) -> p c t i", i=4, t=PACK), raw.rearrange("p t (c i) -> p c t i", i=4))
+            got["wg%d" % c] = g
 
-        def score(c, cs, words, scales):
+        def gp_copy(dst, src):
+            nc.gpsimd.tensor_scalar(dst, src, 1.0, 0.0, ALU.mult, ALU.add)
+
+        def quantise(name, n):
+            codes = sb(name + "_c", [P, n], U32)
+            scales = sb(name + "_s", [P, n], U8)
+            nc.vector.quantize_mx(out=codes[:].bitcast(FP8X4), scales=scales[:], in_=got[name][:])
+            got[name + "q"] = (codes, scales)
+
+        def score(c):
+            quantise("wg%d" % c, P)
+            cs = got["wg%dq" % c]
+            words, scales = (got["key_gw"], got["key_gs"]) if c == NCH else (got["tab_gw"], got["tab_gs"])
             nc.tensor.matmul_mx(out=banks[c][:], lhsT=cs[0][:].bitcast(FP8X4), lhsT_scale=cs[1][:],
                                 rhs=words[:].bitcast(FP4X4), rhs_scale=scales[:], start=True, stop=True)
 
-        def expo(c, scale):
-            e = sb("e%d" % c, [P, PACK, P], F32)
-            nc.scalar.activation(e[:], banks[c][:].rearrange("p (m t) -> p t m", t=PACK), ACT.Exp, scale=scale)
-            return e
+        def expo(c):
+            dst = es[c // 2][:, :, (c % 2) * P : (c % 2 + 1) * P]
+            scale = 1.0 if c == NCH else temp[:, c : c + 1]
+            nc.scalar.activation(dst, banks[c][:].rearrange("p (m t) -> p t m", t=PACK), ACT.Exp, scale=scale)
 
-        def group_sum(c, e):
-            s = sb("s%d" % c, [P, G], F32)
-            nc.vector.tensor_reduce(s[:], e[:].rearrange("p t (g h) -> p g t h", h=2), AX.XY, ALU.add)
-            return s
+        def copy_a():
+            nc.scalar.copy(es[2][:, :, P : 2 * P], banks[NCH][:].rearrange("p (m t) -> p t m", t=PACK))
 
-        def turn(c, e, factor):
+        def pe_sums(u):
+            for k in range(8):
+                t, h = divmod(k, 2)
+                nc.tensor.matmul(sums[u][:, 0:P], es[u][:, t, h : 2 * P : 2], ident[:], start=(k == 0), stop=(k == 7), is_transpose=True)
+            st = sb("st%d" % u, [P, P], F32)
+            nc.scalar.copy(st[:], sums[u][:, 0:P])
+            nc.tensor.transpose(sums[u][:, P : 2 * P], st[:], ident[:])
+            got["sum%d" % u] = sums[u][:, P : 2 * P].rearrange("p (c g) -> p c g", c=2)
+
+        def v_sum(c):
+            src = es[c // 2][:, :, (c % 2) * P : (c % 2 + 1) * P]
+            nc.vector.tensor_reduce(gs[c // 2][:, c % 2, :], src.rearrange("p t (g h) -> p g t h", h=2), AX.XY, ALU.add)
+            got["sum%d" % (c // 2)] = gs[c // 2][:]
+
+        def v_sum_a():
+            nc.vector.tensor_reduce(gs[2][:, 1, :], banks[NCH][:].rearrange("p (g u) -> p g u", u=8), AX.X, ALU.add)
+
+        def turn(u):
             for t in range(PACK):
-                nc.tensor.transpose(banks[c][:, t * P : (t + 1) * P], e[:, t, :], ident[:])
-            v = sb("v%d" % c, [P, PACK, P], F32)
+                base = (t % 2) * 2 * P
+                for c in range(2):
+                    nc.tensor.transpose(banks[2 * u + t // 2][:, base + c * P : base + (c + 1) * P], es[u][:, t, c * P : (c + 1) * P], ident[:])
             for t in range(PACK):
-                nc.scalar.activation(v[:, t, :], banks[c][:, t * P : (t + 1) * P], ACT.Copy, scale=factor[:, t : t + 1])
-            return v
+                base = (t % 2) * 2 * P
+                nc.scalar.activation(vv[u][:, t, :], banks[2 * u + t // 2][:, base : base + 2 * P], ACT.Copy, scale=vs4[:, t : t + 1])
 
-        def finish(c, v):
-            g = sb("f%d" % c, [P, P * PACK], BF16)
-            nc.vector.tensor_tensor(
+        def turn1(c):
+            u, c2 = divmod(c, 2)
+            for t in range(PACK):
+                nc.tensor.transpose(banks[c][:, t * P : (t + 1) * P], es[u][:, t, c2 * P : (c2 + 1) * P], ident[:])
+            for t in range(PACK):
+                nc.scalar.activation(vv[u][:, t, c2 * P : (c2 + 1) * P], banks[c][:, t * P : (t + 1) * P], ACT.Copy, scale=vs4[:, t : t + 1])
+
+        def g_sum(c):
+            src = es[c // 2][:, :, (c % 2) * P : (c % 2 + 1) * P]
+            half = sb("half%d" % c, [P, 2, P], F32)
+            four = sb("four%d" % c, [P, G, 2], F32)
+            nc.gpsimd.tensor_tensor(half[:], src[:, 0:2, :], src[:, 2:4, :], ALU.add)
+            nc.gpsimd.tensor_tensor(four[:].rearrange("p g h -> p (g h)"), half[:, 0, :], half[:, 1, :], ALU.add)
+            nc.gpsimd.tensor_tensor(gs[c // 2][:, c % 2, :], four[:, :, 0], four[:, :, 1], ALU.add)
+            got["sum%d" % (c // 2)] = gs[c // 2][:]
+
+        def turn_w():
+            for t in range(PACK):
+                nc.tensor.transpose(banks[NCH][:, t * P : (t + 1) * P], es[2][:, t, 0:P], ident[:])
+            for t in range(PACK):
+                nc.scalar.activation(vw[:, t, :], banks[NCH][:, t * P : (t + 1) * P], ACT.Copy, scale=os_t[:, t : t + 1])
+
+        def norm(c0, n):
+            u, c2 = divmod(c0, 2)
+            nc.vector.reciprocal(recs[:, c0 : c0 + n, 1 : 2 * G + 1 : 2], got["sum%d" % u][:, c2 : c2 + n, :])
+            for c in range(c0, c0 + n):
+                dst = banks[2 * u + NB(c)][:, (c % 2) * P : (c % 2 + 1) * P]
+                nc.tensor.matmul(dst, recs[:, c, 1 : P + 1], ident[:], start=True, stop=False, is_transpose=True)
+                nc.tensor.matmul(dst, recs[:, c, 0:P], ident[:], start=False, stop=True, is_transpose=True)
+
+        def soft_a():
+            nc.vector.tensor_scalar(nms[:], got["sum2"][:, 1, :], nshp[:, 0:1], 3.0e38, ALU.mult, ALU.min, accum_out=low[:])
+            nc.scalar.activation(pg[:], nms[:], ACT.Exp, bias=low[:, 0:1], scale=-1.0, accum_out=z[:])
+
+        def recip_s():
+            nc.vector.reciprocal(rs[:], got["sum2"][:, 0, :])
+
+        def share():
+            nc.vector.reciprocal(rz[:], z[:])
+            nc.vector.scalar_tensor_tensor(sh[:], pg[:].unsqueeze(2).to_broadcast([P, G, 2]), rz[:, 0:1],
+                                           rs[:].unsqueeze(2).to_broadcast([P, G, 2]), ALU.mult, ALU.mult)
+            nc.tensor.transpose(banks[NCH][:, 0:P], sh[:].rearrange("p g h -> p (g h)"), ident[:])
+
+        def finish(name, v, nrm, n, eng):
+            g = sb(name, [P, n * PACK], BF16)
+            if eng is not nc.vector:
+                held_norm = sb(name + "_n", [P, n], F32)
+                nc.scalar.copy(held_norm[:], nrm)
+                nrm = held_norm[:]
+            eng.tensor_tensor(
                 g[:].rearrange("p (c i t) -> p c t i", i=4, t=PACK),
-                v[:].rearrange("p t (c i) -> p c t i", i=4),
-                banks[c][:, 0:P].rearrange("p (c i) -> p c i", i=4).unsqueeze(2).to_broadcast([P, P // 4, PACK, 4]),
+                v.rearrange("p t (c i) -> p c t i", i=4),
+                nrm.rearrange("p (c i) -> p c i", i=4).unsqueeze(2).to_broadcast([P, n // 4, PACK, 4]),
                 ALU.mult,
             )
-            return quantise("fq%d" % c, g)
+            got[name] = g
 
-        def hidden_norm(c, s):
-            nc.vector.reciprocal(recs[:, c, 1 : 2 * G + 1 : 2], s[:])
-            nc.tensor.matmul(banks[c][:, 0:P], recs[:, c, 1 : P + 1], ident[:], start=True, stop=False, is_transpose=True)
-            nc.tensor.matmul(banks[c][:, 0:P], recs[:, c, 0:P], ident[:], start=False, stop=True, is_transpose=True)
+        def fin(c0, n, eng=nc.vector):
+            u, c2 = divmod(c0, 2)
+            finish("f%d" % c0, vv[u][:, :, c2 * P : (c2 + n) * P], banks[2 * u + NB(c0)][:, c2 * P : (c2 + n) * P], n * P, eng)
 
-        def result(c, wq, hq):
-            nc.tensor.matmul_mx(out=banks[c][:, P : 2 * P], lhsT=wq[0][:].bitcast(FP8X4), lhsT_scale=wq[1][:],
+        def fin_w(eng=nc.vector):
+            finish("fw", vw[:], banks[NCH][:, 0:P], P, eng)
+
+        def result(c0, n, bank, copy=nc.scalar.copy):
+            wq = got["fwq"]
+            hq = got["f%dq" % c0]
+            nc.tensor.matmul_mx(out=bank[:, 0 : n * P], lhsT=wq[0][:].bitcast(FP8X4), lhsT_scale=wq[1][:],
                                 rhs=hq[0][:].bitcast(FP8X4), rhs_scale=hq[1][:], start=True, stop=True)
-            o = sb("o%d" % c, [P, P], F32)
-            nc.scalar.copy(o[:], banks[c][:, P : 2 * P])
-            nc.sync.dma_start(out[:, c * P : (c + 1) * P], o[:])
+            o = sb("o%d" % c0, [P, n * P], F32)
+            copy(o[:], bank[:, 0 : n * P])
+            nc.sync.dma_start(out[:, c0 * P : (c0 + n) * P], o[:])
 
-        tab_gs = gather("tab_gs", tab_s, U8)
-        tab_gw = gather("tab_gw", tab_w, U16)
-        es = {}
-        for c in range(2):
-            wq = quantise("wq%d" % c, weave("wg%d" % c, w_raw[0][:, :, c * P : (c + 1) * P]))
-            score(c, wq, tab_gw, tab_gs)
-            es[c] = expo(c, temp[:, c : c + 1])
-        key_gs = gather("key_gs", key_s, U8)
-        key_gw = gather("key_gw", key_w, U16)
-        qq = quantise("qq", weave("qg", q_raw[:]))
-        score(NCH, qq, key_gw, key_gs)
-        es[NCH] = expo(NCH, 1.0)
-        for c in range(2, NCH):
-            wq = quantise("wq%d" % c, weave("wg%d" % c, w_raw[1][:, :, (c - 2) * P : (c - 1) * P]))
-            score(c, wq, tab_gw, tab_gs)
-            es[c] = expo(c, temp[:, c : c + 1])
+        def NB(c):
+            return 1 if c in (0, 1, 3) else 0
 
-        s0 = group_sum(0, es[0])
-        v0 = turn(0, es[0], vs4)
-        hidden_norm(0, s0)
-
-        sa = sb("sa", [P, G], F32)
-        nc.vector.tensor_reduce(sa[:], banks[NCH][:].rearrange("p (g u) -> p g u", u=8), AX.X, ALU.add)
-        sp = group_sum(NCH, es[NCH])
-        nms = sb("nms", [P, G], F32)
-        low = sb("low", [P, 1], F32)
-        nc.vector.tensor_scalar(nms[:], sa[:], nshp[:, 0:1], 3.0e38, ALU.mult, ALU.min, accum_out=low[:])
-        pg = sb("pg", [P, G], F32)
-        z = sb("z", [P, 1], F32)
-        nc.scalar.activation(pg[:], nms[:], ACT.Exp, bias=low[:, 0:1], scale=-1.0, accum_out=z[:])
-        vw = turn(NCH, es[NCH], os_t)
-        rs = sb("rs", [P, G], F32)
-        nc.vector.reciprocal(rs[:], sp[:])
-        hq0 = finish(0, v0)
-        rz = sb("rz", [P, 1], F32)
-        nc.vector.reciprocal(rz[:], z[:])
-        s1 = group_sum(1, es[1])
-        v1 = turn(1, es[1], vs4)
-        sh = sb("sh", [P, G, 2], F32)
-        nc.vector.scalar_tensor_tensor(sh[:], pg[:].unsqueeze(2).to_broadcast([P, G, 2]), rz[:, 0:1],
-                                       rs[:].unsqueeze(2).to_broadcast([P, G, 2]), ALU.mult, ALU.mult)
-        nc.tensor.transpose(banks[NCH][:, 0:P], sh[:].rearrange("p g h -> p (g h)"), ident[:])
-        hidden_norm(1, s1)
-        s2 = group_sum(2, es[2])
-        v2 = turn(2, es[2], vs4)
-        wq = finish(NCH, vw)
-        result(0, wq, hq0)
-        hq1 = finish(1, v1)
-        result(1, wq, hq1)
-        hidden_norm(2, s2)
-        s3 = group_sum(3, es[3])
-        v3 = turn(3, es[3], vs4)
-        hidden_norm(3, s3)
-        hq2 = finish(2, v2)
-        result(2, wq, hq2)
-        hq3 = finish(3, v3)
-        result(3, wq, hq3)
+        V = nc.vector.tensor_copy
+        S = nc.scalar.copy
+        gather("tab_gs", tab_s, U8)
+        gather("tab_gw", tab_w, U16)
+        weave(0, V)
+        weave(1, S)
+        weave(4, S)
+        weave(2, S)
+        score(0)
+        score(1)
+        gather("key_gw", key_w, U16)
+        gather("key_gs", key_s, U8)
+        expo(0)
+        expo(1)
+        score(4)
+        score(2)
+        weave(3, S)
+        expo(4)
+        v_sum(4)
+        v_sum_a()
+        soft_a()
+        turn_w()
+        score(3)
+        expo(2)
+        v_sum(0)
+        v_sum(1)
+        turn1(0)
+        turn1(1)
+        norm(0, 2)
+        recip_s()
+        expo(3)
+        share()
+        fin(0, 2)
+        v_sum(2)
+        turn1(2)
+        norm(2, 1)
+        v_sum(3)
+        turn1(3)
+        fin_w()
+        norm(3, 1)
+        quantise("f0", 2 * P)
+        quantise("fw", P)
+        result(0, 2, sums[0])
+        fin(2, 1)
+        quantise("f2", P)
+        result(2, 1, sums[1])
+        fin(3, 1)
+        quantise("f3", P)
+        result(3, 1, sums[2])

@@ -17,23 +17,32 @@ AX = mybir.AxisListType
 
 P = 128
 PACK = 4
+K = P * PACK
 T = 2048
 I = 512
 R = 512
 Q = 128
 G = 64
-NCH = R // P
-FLOPS = 2 * (512 * Q * I + 512 * R * I + I * Q * R)
+GROUP = I // G
+HIDDEN_TILES = R // P
+QUERY_TILE = HIDDEN_TILES
+SCALE_ROWS = K // 32
+RUN = 4
+REC_WIDTH = P + 16
+LARGE = 3.0e38
+FLOPS = 2 * (K * Q * I + K * R * I + I * Q * R)
 
 
-def tile_attend_lrshared_bygroup_kernel(tc, query, keys_words, keys_scales, sharp, tab_words, tab_scales, w1, temper, os_in, vs_in, offs, out):
+def tile_attend_lrshared_bygroup_kernel(
+    tc, query, keys_words, keys_scales, sharp, tab_words, tab_scales, w1, temper, os_in, vs_in, offs, out
+):
     nc = tc.nc
     with ExitStack() as ctx:
         held = ctx.enter_context(tc.tile_pool(name="held", bufs=1))
         psum = ctx.enter_context(tc.psum_pool(name="psum", bufs=1))
 
-        def sb(name, shape, dt):
-            return held.tile(shape, dt, name=name, align_bytes=64)
+        def sb(name, shape, dtype):
+            return held.tile(shape, dtype, name=name, align_bytes=64)
 
         offsets = held.tile([P, I // 16], U16, name="offsets")
         tab_w = sb("tab_w", [P, T], U16)
@@ -42,237 +51,190 @@ def tile_attend_lrshared_bygroup_kernel(tc, query, keys_words, keys_scales, shar
         key_s = sb("key_s", [P, T], U8)
         w_raw = [sb("w_raw%d" % h, [P, PACK, 2 * P], F32) for h in range(2)]
         q_raw = sb("q_raw", [P, PACK, Q], F32)
-        temp = sb("temp", [P, NCH], F32)
-        shp = sb("shp", [P, 1], F32)
+        temper_t = sb("temper_t", [P, HIDDEN_TILES], F32)
+        sharp_t = sb("sharp_t", [P, 1], F32)
         vs_t = sb("vs_t", [P, PACK], F32)
         os_t = sb("os_t", [P, PACK], F32)
-        vs4 = sb("vs4", [P, PACK], F32)
-        nshp = sb("nshp", [P, 1], F32)
         ident = sb("ident", [P, P], F32)
-        recs = sb("recs", [P, NCH, 2 * G + 16], F32)
-        w1v = w1.rearrange("(p j) r -> p j r", j=PACK)
+        recs = sb("recs", [P, HIDDEN_TILES, REC_WIDTH], F32)
+
         nc.gpsimd.memset(tab_s[:].bitcast(I32), 0)
         nc.vector.memset(recs[:], 0.0)
         nc.vector.memset(key_s[:].bitcast(I32), 0)
         make_identity(nc, ident[:])
+
+        def load_scale_rows(plane, scales):
+            for j in range(4):
+                nc.scalar.dma_start(plane[j:P:32, :].bitcast(I32), scales[0, j:SCALE_ROWS:4, :].bitcast(I32))
+
+        w1_rows = w1.rearrange("(p j) r -> p j r", j=PACK)
         nc.sync.dma_start(offsets[:], offs)
-        nc.scalar.dma_start(shp[:], sharp)
-        for j in range(4):
-            nc.scalar.dma_start(tab_s[j:P:32, :].bitcast(I32), tab_scales[0, j:16:4, :].bitcast(I32))
-        nc.sync.dma_start(vs_t[:], vs_in.rearrange("o (p t) -> p (o t)", t=PACK))
+        load_scale_rows(tab_s, tab_scales)
         nc.sync.dma_start(tab_w[:].bitcast(I32), tab_words[0].bitcast(I32))
-        nc.sync.dma_start(w_raw[0][:], w1v[:, :, 0 : 2 * P])
-        nc.sync.dma_start(q_raw[:], query.rearrange("(p j) q -> p j q", j=PACK))
-        nc.sync.dma_start(w_raw[1][:], w1v[:, :, 2 * P : 4 * P])
-        with nc.allow_non_contiguous_dma(reason="one value a partition"):
-            nc.sync.dma_start(temp[:], temper.rearrange("(c p) o -> p (c o)", p=P))
-        for j in range(4):
-            nc.scalar.dma_start(key_s[j:P:32, :].bitcast(I32), keys_scales[0, j:16:4, :].bitcast(I32))
+        nc.sync.dma_start(w_raw[0][:], w1_rows[:, :, 0 : 2 * P])
+        with nc.allow_non_contiguous_dma(reason="one temper a partition for each hidden tile"):
+            nc.scalar.dma_start(temper_t[:], temper.rearrange("(c p) o -> p (c o)", p=P))
         nc.sync.dma_start(key_w[:].bitcast(I32), keys_words[0].bitcast(I32))
+        nc.sync.dma_start(q_raw[:], query.rearrange("(p j) q -> p j q", j=PACK))
+        nc.sync.dma_start(w_raw[1][:], w1_rows[:, :, 2 * P : 4 * P])
+        load_scale_rows(key_s, keys_scales)
+        nc.sync.dma_start(vs_t[:], vs_in.rearrange("o (p t) -> p (o t)", t=PACK))
+        nc.sync.dma_start(sharp_t[:], sharp)
         nc.sync.dma_start(os_t[:], os_in.rearrange("o (p t) -> p (o t)", t=PACK))
-        nc.gpsimd.tensor_scalar(vs4[:], vs_t[:], 4.0, 0.0, ALU.mult, ALU.add)
-        nc.gpsimd.tensor_scalar(nshp[:], shp[:], -0.125, 0.0, ALU.mult, ALU.add)
 
-        banks = [psum.tile([P, I], F32, name="bank%d" % c) for c in range(NCH + 1)]
-        sums = [psum.tile([P, 2 * P], F32, name="sums%d" % u) for u in range(3)]
-        es = [sb("e%d" % u, [P, PACK, 2 * P], F32) for u in range(3)]
-        vv = [sb("v%d" % u, [P, PACK, 2 * P], F32) for u in range(2)]
-        vw = sb("vw", [P, PACK, P], F32)
-        gs = [sb("gs%d" % u, [P, 2, G], F32) for u in range(3)]
-        nms = sb("nms", [P, G], F32)
-        low = sb("low", [P, 1], F32)
-        pg = sb("pg", [P, G], F32)
-        z = sb("z", [P, 1], F32)
-        rs = sb("rs", [P, G], F32)
-        rz = sb("rz", [P, 1], F32)
-        sh = sb("sh", [P, G, 2], F32)
-        got = {}
+        vs4 = sb("vs4", [P, PACK], F32)
+        nc.scalar.activation(vs4[:], vs_t[:], ACT.Copy, scale=4.0)
+        neg_sharp = sb("neg_sharp", [P, 1], F32)
+        nc.scalar.activation(neg_sharp[:], sharp_t[:], ACT.Copy, scale=-1.0 / GROUP)
 
-        def tagged(name, shape, dt, tag):
-            return held.tile(shape, dt, name=name, tag=tag or name, align_bytes=64)
+        banks = [psum.tile([P, I], F32, name="bank%d" % c) for c in range(HIDDEN_TILES + 1)]
 
-        def gather(name, window, dt, tag=None):
-            got[name] = tagged(name, [P, I], dt, tag)
-            nc.vector.tensor_copy(got[name][:], window[:].indirect(offsets[:]))
+        def gather(name, window, dtype):
+            picked = sb(name, [P, I], dtype)
+            nc.vector.tensor_copy(picked[:], window[:].indirect(offsets[:]))
+            return picked
 
-        def weave(c, copy, tag=None):
-            raw = q_raw[:] if c == NCH else w_raw[c // 2][:, :, (c % 2) * P : (c % 2 + 1) * P]
-            g = tagged("wg%d" % c, [P, P * PACK], BF16, tag)
-            copy(g[:].rearrange("p (c i t) -> p c t i", i=4, t=PACK), raw.rearrange("p t (c i) -> p c t i", i=4))
-            got["wg%d" % c] = g
+        def by_place(planes):
+            return planes.rearrange("p t (c i) -> p c t i", i=RUN)
 
-        def gp_copy(dst, src):
-            nc.gpsimd.tensor_scalar(dst, src, 1.0, 0.0, ALU.mult, ALU.add)
+        def woven(words):
+            return words.rearrange("p (c i t) -> p c t i", i=RUN, t=PACK)
 
-        def quantise(name, n):
-            codes = sb(name + "_c", [P, n], U32)
-            scales = sb(name + "_s", [P, n], U8)
-            nc.vector.quantize_mx(out=codes[:].bitcast(FP8X4), scales=scales[:], in_=got[name][:])
-            got[name + "q"] = (codes, scales)
+        def quantise(name, values, columns):
+            codes = sb(name + "_codes", [P, columns], U32)
+            scales = sb(name + "_scales", [P, columns], U8)
+            nc.vector.quantize_mx(out=codes[:].bitcast(FP8X4), scales=scales[:], in_=values[:])
+            return codes, scales
 
-        def score(c):
-            quantise("wg%d" % c, P)
-            cs = got["wg%dq" % c]
-            words, scales = (got["key_gw"], got["key_gs"]) if c == NCH else (got["tab_gw"], got["tab_gs"])
-            nc.tensor.matmul_mx(out=banks[c][:], lhsT=cs[0][:].bitcast(FP8X4), lhsT_scale=cs[1][:],
-                                rhs=words[:].bitcast(FP4X4), rhs_scale=scales[:], start=True, stop=True)
+        tab_gs = gather("tab_gs", tab_s, U8)
+        tab_gw = gather("tab_gw", tab_w, U16)
+        key_gw = gather("key_gw", key_w, U16)
+        key_gs = gather("key_gs", key_s, U8)
 
-        def expo(c):
-            dst = es[c // 2][:, :, (c % 2) * P : (c % 2 + 1) * P]
-            scale = 1.0 if c == NCH else temp[:, c : c + 1]
-            nc.scalar.activation(dst, banks[c][:].rearrange("p (m t) -> p t m", t=PACK), ACT.Exp, scale=scale)
+        tile_order = [0, 1, QUERY_TILE, 2, 3]
 
-        def copy_a():
-            nc.scalar.copy(es[2][:, :, P : 2 * P], banks[NCH][:].rearrange("p (m t) -> p t m", t=PACK))
+        stationary = {}
+        for c in tile_order:
+            raw = q_raw[:] if c == QUERY_TILE else w_raw[c // 2][:, :, (c % 2) * P : (c % 2 + 1) * P]
+            stationary[c] = sb("stationary%d" % c, [P, K], BF16)
+            copy = nc.vector.tensor_copy if c == 0 else nc.scalar.copy
+            copy(woven(stationary[c][:]), by_place(raw))
 
-        def pe_sums(u):
-            for k in range(8):
-                t, h = divmod(k, 2)
-                nc.tensor.matmul(sums[u][:, 0:P], es[u][:, t, h : 2 * P : 2], ident[:], start=(k == 0), stop=(k == 7), is_transpose=True)
-            st = sb("st%d" % u, [P, P], F32)
-            nc.scalar.copy(st[:], sums[u][:, 0:P])
-            nc.tensor.transpose(sums[u][:, P : 2 * P], st[:], ident[:])
-            got["sum%d" % u] = sums[u][:, P : 2 * P].rearrange("p (c g) -> p c g", c=2)
+        for c in tile_order:
+            codes, scales = quantise("stationary%d" % c, stationary[c], P)
+            words, word_scales = (key_gw, key_gs) if c == QUERY_TILE else (tab_gw, tab_gs)
+            nc.tensor.matmul_mx(
+                out=banks[c][:],
+                lhsT=codes[:].bitcast(FP8X4),
+                lhsT_scale=scales[:],
+                rhs=words[:].bitcast(FP4X4),
+                rhs_scale=word_scales[:],
+                start=True,
+                stop=True,
+            )
 
-        def v_sum(c):
-            src = es[c // 2][:, :, (c % 2) * P : (c % 2 + 1) * P]
-            nc.vector.tensor_reduce(gs[c // 2][:, c % 2, :], src.rearrange("p t (g h) -> p g t h", h=2), AX.XY, ALU.add)
-            got["sum%d" % (c // 2)] = gs[c // 2][:]
+        exps = {}
+        for c in tile_order:
+            exps[c] = sb("exps%d" % c, [P, PACK, P], F32)
+            scale = 1.0 if c == QUERY_TILE else temper_t[:, c : c + 1]
+            nc.scalar.activation(exps[c][:], banks[c][:].rearrange("p (m t) -> p t m", t=PACK), ACT.Exp, scale=scale)
 
-        def v_sum_a():
-            nc.vector.tensor_reduce(gs[2][:, 1, :], banks[NCH][:].rearrange("p (g u) -> p g u", u=8), AX.X, ALU.add)
+        def group_sums_on_vector(c, sums):
+            nc.vector.tensor_reduce(sums, exps[c][:].rearrange("p t (g h) -> p g t h", h=2), AX.XY, ALU.add)
 
-        def turn(u):
-            for t in range(PACK):
-                base = (t % 2) * 2 * P
-                for c in range(2):
-                    nc.tensor.transpose(banks[2 * u + t // 2][:, base + c * P : base + (c + 1) * P], es[u][:, t, c * P : (c + 1) * P], ident[:])
-            for t in range(PACK):
-                base = (t % 2) * 2 * P
-                nc.scalar.activation(vv[u][:, t, :], banks[2 * u + t // 2][:, base : base + 2 * P], ACT.Copy, scale=vs4[:, t : t + 1])
-
-        def turn1(c):
-            u, c2 = divmod(c, 2)
-            for t in range(PACK):
-                nc.tensor.transpose(banks[c][:, t * P : (t + 1) * P], es[u][:, t, c2 * P : (c2 + 1) * P], ident[:])
-            for t in range(PACK):
-                nc.scalar.activation(vv[u][:, t, c2 * P : (c2 + 1) * P], banks[c][:, t * P : (t + 1) * P], ACT.Copy, scale=vs4[:, t : t + 1])
-
-        def g_sum(c):
-            src = es[c // 2][:, :, (c % 2) * P : (c % 2 + 1) * P]
+        def group_sums_on_gpsimd(c, sums):
             half = sb("half%d" % c, [P, 2, P], F32)
-            four = sb("four%d" % c, [P, G, 2], F32)
-            nc.gpsimd.tensor_tensor(half[:], src[:, 0:2, :], src[:, 2:4, :], ALU.add)
-            nc.gpsimd.tensor_tensor(four[:].rearrange("p g h -> p (g h)"), half[:, 0, :], half[:, 1, :], ALU.add)
-            nc.gpsimd.tensor_tensor(gs[c // 2][:, c % 2, :], four[:, :, 0], four[:, :, 1], ALU.add)
-            got["sum%d" % (c // 2)] = gs[c // 2][:]
+            quarter = sb("quarter%d" % c, [P, G, 2], F32)
+            nc.gpsimd.tensor_tensor(half[:], exps[c][:, 0:2, :], exps[c][:, 2:4, :], ALU.add)
+            nc.gpsimd.tensor_tensor(quarter[:].rearrange("p g h -> p (g h)"), half[:, 0, :], half[:, 1, :], ALU.add)
+            nc.gpsimd.tensor_tensor(sums, quarter[:, :, 0], quarter[:, :, 1], ALU.add)
 
-        def turn_w():
+        def turn(c, planes, slot_factor):
             for t in range(PACK):
-                nc.tensor.transpose(banks[NCH][:, t * P : (t + 1) * P], es[2][:, t, 0:P], ident[:])
+                nc.tensor.transpose(banks[c][:, t * P : (t + 1) * P], exps[c][:, t, :], ident[:])
             for t in range(PACK):
-                nc.scalar.activation(vw[:, t, :], banks[NCH][:, t * P : (t + 1) * P], ACT.Copy, scale=os_t[:, t : t + 1])
+                nc.scalar.activation(
+                    planes[:, t, :], banks[c][:, t * P : (t + 1) * P], ACT.Copy, scale=slot_factor[:, t : t + 1]
+                )
 
-        def norm(c0, n):
-            u, c2 = divmod(c0, 2)
-            nc.vector.reciprocal(recs[:, c0 : c0 + n, 1 : 2 * G + 1 : 2], got["sum%d" % u][:, c2 : c2 + n, :])
-            for c in range(c0, c0 + n):
-                dst = banks[2 * u + NB(c)][:, (c % 2) * P : (c % 2 + 1) * P]
-                nc.tensor.matmul(dst, recs[:, c, 1 : P + 1], ident[:], start=True, stop=False, is_transpose=True)
-                nc.tensor.matmul(dst, recs[:, c, 0:P], ident[:], start=False, stop=True, is_transpose=True)
-
-        def soft_a():
-            nc.vector.tensor_scalar(nms[:], got["sum2"][:, 1, :], nshp[:, 0:1], 3.0e38, ALU.mult, ALU.min, accum_out=low[:])
-            nc.scalar.activation(pg[:], nms[:], ACT.Exp, bias=low[:, 0:1], scale=-1.0, accum_out=z[:])
-
-        def recip_s():
-            nc.vector.reciprocal(rs[:], got["sum2"][:, 0, :])
-
-        def share():
-            nc.vector.reciprocal(rz[:], z[:])
-            nc.vector.scalar_tensor_tensor(sh[:], pg[:].unsqueeze(2).to_broadcast([P, G, 2]), rz[:, 0:1],
-                                           rs[:].unsqueeze(2).to_broadcast([P, G, 2]), ALU.mult, ALU.mult)
-            nc.tensor.transpose(banks[NCH][:, 0:P], sh[:].rearrange("p g h -> p (g h)"), ident[:])
-
-        def finish(name, v, nrm, n, eng):
-            g = sb(name, [P, n * PACK], BF16)
-            if eng is not nc.vector:
-                held_norm = sb(name + "_n", [P, n], F32)
-                nc.scalar.copy(held_norm[:], nrm)
-                nrm = held_norm[:]
-            eng.tensor_tensor(
-                g[:].rearrange("p (c i t) -> p c t i", i=4, t=PACK),
-                v.rearrange("p t (c i) -> p c t i", i=4),
-                nrm.rearrange("p (c i) -> p c i", i=4).unsqueeze(2).to_broadcast([P, n // 4, PACK, 4]),
+        def finish(name, planes, row_factor, columns):
+            values = sb(name, [P, columns * PACK], BF16)
+            nc.vector.tensor_tensor(
+                woven(values[:]),
+                by_place(planes[:]),
+                row_factor.rearrange("p (c i) -> p c i", i=RUN).unsqueeze(2).to_broadcast([P, columns // RUN, PACK, RUN]),
                 ALU.mult,
             )
-            got[name] = g
+            return quantise(name, values, columns)
 
-        def fin(c0, n, eng=nc.vector):
-            u, c2 = divmod(c0, 2)
-            finish("f%d" % c0, vv[u][:, :, c2 * P : (c2 + n) * P], banks[2 * u + NB(c0)][:, c2 * P : (c2 + n) * P], n * P, eng)
+        def hidden_sums(first, count):
+            mz = sb("mz%d" % first, [P, count, G], F32)
+            planes = sb("h_planes%d" % first, [P, PACK, count * P], F32)
+            for n in range(count):
+                group_sums_on_vector(first + n, mz[:, n, :])
+            for n in range(count):
+                turn(first + n, planes[:, :, n * P : (n + 1) * P], vs4)
+            nc.vector.reciprocal(recs[:, first : first + count, 1 : P + 1 : 2], mz[:])
+            factor_bank = banks[first + count - 1]
+            for n in range(count):
+                dst = factor_bank[:, n * P : (n + 1) * P]
+                nc.tensor.matmul(dst, recs[:, first + n, 1 : P + 1], ident[:], start=True, stop=False, is_transpose=True)
+                nc.tensor.matmul(dst, recs[:, first + n, 0:P], ident[:], start=False, stop=True, is_transpose=True)
+            return planes
 
-        def fin_w(eng=nc.vector):
-            finish("fw", vw[:], banks[NCH][:, 0:P], P, eng)
+        def hidden_finish(first, count, planes):
+            return finish("ht1_%d" % first, planes, banks[first + count - 1][:, 0 : count * P], count * P)
 
-        def result(c0, n, bank, copy=nc.scalar.copy):
-            wq = got["fwq"]
-            hq = got["f%dq" % c0]
-            nc.tensor.matmul_mx(out=bank[:, 0 : n * P], lhsT=wq[0][:].bitcast(FP8X4), lhsT_scale=wq[1][:],
-                                rhs=hq[0][:].bitcast(FP8X4), rhs_scale=hq[1][:], start=True, stop=True)
-            o = sb("o%d" % c0, [P, n * P], F32)
-            copy(o[:], bank[:, 0 : n * P])
-            nc.sync.dma_start(out[:, c0 * P : (c0 + n) * P], o[:])
+        def result(first, count, ht):
+            columns = count * P
+            out_bank = psum.tile([P, columns], F32, name="out_bank%d" % first)
+            nc.tensor.matmul_mx(
+                out=out_bank[:],
+                lhsT=wt_codes[:].bitcast(FP8X4),
+                lhsT_scale=wt_scales[:],
+                rhs=ht[0][:].bitcast(FP8X4),
+                rhs_scale=ht[1][:],
+                start=True,
+                stop=True,
+            )
+            staged = sb("result%d" % first, [P, columns], F32)
+            nc.scalar.copy(staged[:], out_bank[:])
+            nc.sync.dma_start(out[:, first * P : first * P + columns], staged[:])
 
-        def NB(c):
-            return 1 if c in (0, 1, 3) else 0
-
-        V = nc.vector.tensor_copy
-        S = nc.scalar.copy
-        gather("tab_gs", tab_s, U8)
-        gather("tab_gw", tab_w, U16)
-        weave(0, V)
-        weave(1, S)
-        weave(4, S)
-        weave(2, S)
-        score(0)
-        score(1)
-        gather("key_gw", key_w, U16)
-        gather("key_gs", key_s, U8)
-        expo(0)
-        expo(1)
-        score(4)
-        score(2)
-        weave(3, S)
-        expo(4)
-        v_sum(4)
-        v_sum_a()
-        soft_a()
-        turn_w()
-        score(3)
-        expo(2)
-        v_sum(0)
-        v_sum(1)
-        turn1(0)
-        turn1(1)
-        norm(0, 2)
-        recip_s()
-        expo(3)
-        share()
-        fin(0, 2)
-        v_sum(2)
-        turn1(2)
-        norm(2, 1)
-        v_sum(3)
-        turn1(3)
-        fin_w()
-        norm(3, 1)
-        quantise("f0", 2 * P)
-        quantise("fw", P)
-        result(0, 2, sums[0])
-        fin(2, 1)
-        quantise("f2", P)
-        result(2, 1, sums[1])
-        fin(3, 1)
-        quantise("f3", P)
-        result(3, 1, sums[2])
+        p02 = hidden_sums(0, 2)
+        bank_q = banks[QUERY_TILE]
+        s_sums = sb("s_sums", [P, G], F32)
+        group_sums_on_vector(QUERY_TILE, s_sums[:])
+        a_sums = sb("a_sums", [P, G], F32)
+        nc.vector.tensor_reduce(a_sums[:], bank_q[:].rearrange("p (g u) -> p g u", u=GROUP), AX.X, ALU.add)
+        neg_ms = sb("neg_ms", [P, G], F32)
+        neg_max = sb("neg_max", [P, 1], F32)
+        nc.vector.tensor_scalar(neg_ms[:], a_sums[:], neg_sharp[:, 0:1], LARGE, ALU.mult, ALU.min, accum_out=neg_max[:])
+        pg = sb("pg", [P, G], F32)
+        z = sb("z", [P, 1], F32)
+        nc.scalar.activation(pg[:], neg_ms[:], ACT.Exp, bias=neg_max[:, 0:1], scale=-1.0, accum_out=z[:])
+        w_planes = sb("w_planes", [P, PACK, Q], F32)
+        turn(QUERY_TILE, w_planes, os_t)
+        rec_s = sb("rec_s", [P, G], F32)
+        nc.vector.reciprocal(rec_s[:], s_sums[:])
+        rec_z = sb("rec_z", [P, 1], F32)
+        nc.vector.reciprocal(rec_z[:], z[:])
+        sh = sb("sh", [P, G, 2], F32)
+        nc.vector.scalar_tensor_tensor(
+            sh[:],
+            pg[:].unsqueeze(2).to_broadcast([P, G, 2]),
+            rec_z[:, 0:1],
+            rec_s[:].unsqueeze(2).to_broadcast([P, G, 2]),
+            ALU.mult,
+            ALU.mult,
+        )
+        nc.tensor.transpose(bank_q[:, 0:P], sh[:].rearrange("p g h -> p (g h)"), ident[:])
+        p21 = hidden_sums(2, 1)
+        p31 = hidden_sums(3, 1)
+        h02 = hidden_finish(0, 2, p02)
+        wt_codes, wt_scales = finish("wt1", w_planes, bank_q[:, 0:P], Q)
+        result(0, 2, h02)
+        h21 = hidden_finish(2, 1, p21)
+        result(2, 1, h21)
+        h31 = hidden_finish(3, 1, p31)
+        result(3, 1, h31)

from contextlib import ExitStack

import concourse.mybir as mybir
from concourse.masks import make_identity

F32 = mybir.dt.float32
BF16 = mybir.dt.bfloat16
I32 = mybir.dt.int32
U32 = mybir.dt.uint32
U16 = mybir.dt.uint16
U8 = mybir.dt.uint8
FP8X4 = mybir.dt.float8_e4m3fn_x4
FP4X4 = mybir.dt.float4_e2m1fn_x4
ALU = mybir.AluOpType
ACT = mybir.ActivationFunctionType
AX = mybir.AxisListType

P = 128
PACK = 4
K = P * PACK
T = 2048
I = 512
R = 512
Q = 128
G = 64
GROUP = I // G
HIDDEN_TILES = R // P
QUERY_TILE = HIDDEN_TILES
SCALE_ROWS = K // 32
RUN = 4
REC_WIDTH = P + 16
LARGE = 3.0e38
FLOPS = 2 * (K * Q * I + K * R * I + I * Q * R)


def tile_attend_lrshared_bygroup_kernel(
    tc, query, keys_words, keys_scales, sharp, tab_words, tab_scales, w1, temper, os_in, vs_in, offs, out
):
    nc = tc.nc
    with ExitStack() as ctx:
        held = ctx.enter_context(tc.tile_pool(name="held", bufs=1))
        psum = ctx.enter_context(tc.psum_pool(name="psum", bufs=1))

        def sb(name, shape, dtype):
            return held.tile(shape, dtype, name=name, align_bytes=64)

        offsets = held.tile([P, I // 16], U16, name="offsets")
        tab_w = sb("tab_w", [P, T], U16)
        key_w = sb("key_w", [P, T], U16)
        tab_s = sb("tab_s", [P, T], U8)
        key_s = sb("key_s", [P, T], U8)
        w_raw = [sb("w_raw%d" % h, [P, PACK, 2 * P], F32) for h in range(2)]
        q_raw = sb("q_raw", [P, PACK, Q], F32)
        temper_t = sb("temper_t", [P, HIDDEN_TILES], F32)
        sharp_t = sb("sharp_t", [P, 1], F32)
        vs_t = sb("vs_t", [P, PACK], F32)
        os_t = sb("os_t", [P, PACK], F32)
        ident = sb("ident", [P, P], F32)
        recs = sb("recs", [P, HIDDEN_TILES, REC_WIDTH], F32)

        nc.gpsimd.memset(tab_s[:].bitcast(I32), 0)
        nc.vector.memset(recs[:], 0.0)
        nc.vector.memset(key_s[:].bitcast(I32), 0)
        make_identity(nc, ident[:])

        def load_scale_rows(plane, scales):
            for j in range(4):
                nc.scalar.dma_start(plane[j:P:32, :].bitcast(I32), scales[0, j:SCALE_ROWS:4, :].bitcast(I32))

        w1_rows = w1.rearrange("(p j) r -> p j r", j=PACK)
        nc.sync.dma_start(offsets[:], offs)
        load_scale_rows(tab_s, tab_scales)
        nc.sync.dma_start(tab_w[:].bitcast(I32), tab_words[0].bitcast(I32))
        nc.sync.dma_start(w_raw[0][:], w1_rows[:, :, 0 : 2 * P])
        with nc.allow_non_contiguous_dma(reason="one temper a partition for each hidden tile"):
            nc.scalar.dma_start(temper_t[:], temper.rearrange("(c p) o -> p (c o)", p=P))
        nc.sync.dma_start(key_w[:].bitcast(I32), keys_words[0].bitcast(I32))
        nc.sync.dma_start(q_raw[:], query.rearrange("(p j) q -> p j q", j=PACK))
        nc.sync.dma_start(w_raw[1][:], w1_rows[:, :, 2 * P : 4 * P])
        load_scale_rows(key_s, keys_scales)
        nc.sync.dma_start(vs_t[:], vs_in.rearrange("o (p t) -> p (o t)", t=PACK))
        nc.sync.dma_start(sharp_t[:], sharp)
        nc.sync.dma_start(os_t[:], os_in.rearrange("o (p t) -> p (o t)", t=PACK))

        vs4 = sb("vs4", [P, PACK], F32)
        nc.scalar.activation(vs4[:], vs_t[:], ACT.Copy, scale=4.0)
        neg_sharp = sb("neg_sharp", [P, 1], F32)
        nc.scalar.activation(neg_sharp[:], sharp_t[:], ACT.Copy, scale=-1.0 / GROUP)

        banks = [psum.tile([P, I], F32, name="bank%d" % c) for c in range(HIDDEN_TILES + 1)]

        def gather(name, window, dtype):
            picked = sb(name, [P, I], dtype)
            nc.vector.tensor_copy(picked[:], window[:].indirect(offsets[:]))
            return picked

        def by_place(planes):
            return planes.rearrange("p t (c i) -> p c t i", i=RUN)

        def woven(words):
            return words.rearrange("p (c i t) -> p c t i", i=RUN, t=PACK)

        def quantise(name, values, columns):
            codes = sb(name + "_codes", [P, columns], U32)
            scales = sb(name + "_scales", [P, columns], U8)
            nc.vector.quantize_mx(out=codes[:].bitcast(FP8X4), scales=scales[:], in_=values[:])
            return codes, scales

        tab_gs = gather("tab_gs", tab_s, U8)
        tab_gw = gather("tab_gw", tab_w, U16)
        key_gw = gather("key_gw", key_w, U16)
        key_gs = gather("key_gs", key_s, U8)

        tile_order = [0, 1, QUERY_TILE, 2, 3]

        stationary = {}
        for c in tile_order:
            raw = q_raw[:] if c == QUERY_TILE else w_raw[c // 2][:, :, (c % 2) * P : (c % 2 + 1) * P]
            stationary[c] = sb("stationary%d" % c, [P, K], BF16)
            copy = nc.vector.tensor_copy if c == 0 else nc.scalar.copy
            copy(woven(stationary[c][:]), by_place(raw))

        for c in tile_order:
            codes, scales = quantise("stationary%d" % c, stationary[c], P)
            words, word_scales = (key_gw, key_gs) if c == QUERY_TILE else (tab_gw, tab_gs)
            nc.tensor.matmul_mx(
                out=banks[c][:],
                lhsT=codes[:].bitcast(FP8X4),
                lhsT_scale=scales[:],
                rhs=words[:].bitcast(FP4X4),
                rhs_scale=word_scales[:],
                start=True,
                stop=True,
            )

        exps = {}
        for c in tile_order:
            exps[c] = sb("exps%d" % c, [P, PACK, P], F32)
            scale = 1.0 if c == QUERY_TILE else temper_t[:, c : c + 1]
            nc.scalar.activation(exps[c][:], banks[c][:].rearrange("p (m t) -> p t m", t=PACK), ACT.Exp, scale=scale)

        def group_sums_on_vector(c, sums):
            nc.vector.tensor_reduce(sums, exps[c][:].rearrange("p t (g h) -> p g t h", h=2), AX.XY, ALU.add)

        def group_sums_on_gpsimd(c, sums):
            half = sb("half%d" % c, [P, 2, P], F32)
            quarter = sb("quarter%d" % c, [P, G, 2], F32)
            nc.gpsimd.tensor_tensor(half[:], exps[c][:, 0:2, :], exps[c][:, 2:4, :], ALU.add)
            nc.gpsimd.tensor_tensor(quarter[:].rearrange("p g h -> p (g h)"), half[:, 0, :], half[:, 1, :], ALU.add)
            nc.gpsimd.tensor_tensor(sums, quarter[:, :, 0], quarter[:, :, 1], ALU.add)

        def turn(c, planes, slot_factor):
            for t in range(PACK):
                nc.tensor.transpose(banks[c][:, t * P : (t + 1) * P], exps[c][:, t, :], ident[:])
            for t in range(PACK):
                nc.scalar.activation(
                    planes[:, t, :], banks[c][:, t * P : (t + 1) * P], ACT.Copy, scale=slot_factor[:, t : t + 1]
                )

        def finish(name, planes, row_factor, columns):
            values = sb(name, [P, columns * PACK], BF16)
            nc.vector.tensor_tensor(
                woven(values[:]),
                by_place(planes[:]),
                row_factor.rearrange("p (c i) -> p c i", i=RUN).unsqueeze(2).to_broadcast([P, columns // RUN, PACK, RUN]),
                ALU.mult,
            )
            return quantise(name, values, columns)

        def hidden_sums(first, count):
            mz = sb("mz%d" % first, [P, count, G], F32)
            planes = sb("h_planes%d" % first, [P, PACK, count * P], F32)
            for n in range(count):
                group_sums_on_vector(first + n, mz[:, n, :])
            for n in range(count):
                turn(first + n, planes[:, :, n * P : (n + 1) * P], vs4)
            nc.vector.reciprocal(recs[:, first : first + count, 1 : P + 1 : 2], mz[:])
            factor_bank = banks[first + count - 1]
            for n in range(count):
                dst = factor_bank[:, n * P : (n + 1) * P]
                nc.tensor.matmul(dst, recs[:, first + n, 1 : P + 1], ident[:], start=True, stop=False, is_transpose=True)
                nc.tensor.matmul(dst, recs[:, first + n, 0:P], ident[:], start=False, stop=True, is_transpose=True)
            return planes

        def hidden_finish(first, count, planes):
            return finish("ht1_%d" % first, planes, banks[first + count - 1][:, 0 : count * P], count * P)

        def result(first, count, ht):
            columns = count * P
            out_bank = psum.tile([P, columns], F32, name="out_bank%d" % first)
            nc.tensor.matmul_mx(
                out=out_bank[:],
                lhsT=wt_codes[:].bitcast(FP8X4),
                lhsT_scale=wt_scales[:],
                rhs=ht[0][:].bitcast(FP8X4),
                rhs_scale=ht[1][:],
                start=True,
                stop=True,
            )
            staged = sb("result%d" % first, [P, columns], F32)
            nc.scalar.copy(staged[:], out_bank[:])
            nc.sync.dma_start(out[:, first * P : first * P + columns], staged[:])

        p02 = hidden_sums(0, 2)
        bank_q = banks[QUERY_TILE]
        s_sums = sb("s_sums", [P, G], F32)
        group_sums_on_vector(QUERY_TILE, s_sums[:])
        a_sums = sb("a_sums", [P, G], F32)
        nc.vector.tensor_reduce(a_sums[:], bank_q[:].rearrange("p (g u) -> p g u", u=GROUP), AX.X, ALU.add)
        neg_ms = sb("neg_ms", [P, G], F32)
        neg_max = sb("neg_max", [P, 1], F32)
        nc.vector.tensor_scalar(neg_ms[:], a_sums[:], neg_sharp[:, 0:1], LARGE, ALU.mult, ALU.min, accum_out=neg_max[:])
        pg = sb("pg", [P, G], F32)
        z = sb("z", [P, 1], F32)
        nc.scalar.activation(pg[:], neg_ms[:], ACT.Exp, bias=neg_max[:, 0:1], scale=-1.0, accum_out=z[:])
        w_planes = sb("w_planes", [P, PACK, Q], F32)
        turn(QUERY_TILE, w_planes, os_t)
        rec_s = sb("rec_s", [P, G], F32)
        nc.vector.reciprocal(rec_s[:], s_sums[:])
        rec_z = sb("rec_z", [P, 1], F32)
        nc.vector.reciprocal(rec_z[:], z[:])
        sh = sb("sh", [P, G, 2], F32)
        nc.vector.scalar_tensor_tensor(
            sh[:],
            pg[:].unsqueeze(2).to_broadcast([P, G, 2]),
            rec_z[:, 0:1],
            rec_s[:].unsqueeze(2).to_broadcast([P, G, 2]),
            ALU.mult,
            ALU.mult,
        )
        nc.tensor.transpose(bank_q[:, 0:P], sh[:].rearrange("p g h -> p (g h)"), ident[:])
        p21 = hidden_sums(2, 1)
        p31 = hidden_sums(3, 1)
        h02 = hidden_finish(0, 2, p02)
        wt_codes, wt_scales = finish("wt1", w_planes, bank_q[:, 0:P], Q)
        result(0, 2, h02)
        h21 = hidden_finish(2, 1, p21)
        result(2, 1, h21)
        h31 = hidden_finish(3, 1, p31)
        result(3, 1, h31)
